import numpy as np
import ml_dtypes


def mxq(x, axis, fmt="e4m3"):
    dtype, down = {"e4m3": (ml_dtypes.float8_e4m3fn, 7), "e5m2": (ml_dtypes.float8_e5m2, 14)}[fmt]
    v = np.moveaxis(np.asarray(x, np.float32).astype(ml_dtypes.bfloat16).astype(np.float64), axis, -1)
    blocks = v.reshape(v.shape[:-1] + (-1, 32))
    amax = np.abs(blocks).max(-1, keepdims=True)
    byte = np.maximum(np.where(amax > 0, np.frexp(amax)[1] - 1 + 127, 0) - down, 1)
    scale = np.exp2(byte - 127.0)
    codes = (blocks / scale).astype(np.float32).astype(dtype).astype(np.float64)
    return np.moveaxis((codes * scale).reshape(v.shape), -1, axis)


WIDE = False


def mx_kscale(k):
    if not WIDE:
        return np.ones(k)
    levels = np.array([10, -10, 5, -5, 0])
    if k % 512:
        return np.exp2(np.random.permutation(np.resize(levels, k // 32))).repeat(32)
    a = np.empty((k // 512, 16))
    for p in range(k // 512):
        a[p, :8] = np.random.permutation(np.resize(levels, 8))
        for g in range(8):
            far = levels[np.abs(levels - a[p, g]) >= 10]
            a[p, g + 8] = far[np.random.randint(len(far))]
    return np.exp2(a.ravel()).repeat(32)


def f64(x):
    return np.asarray(x).astype(np.float64)


def striped(idx):
    return np.tile(idx.reshape(-1, 16).T, (8, 1)).astype(np.uint16)


def unstriped(offs):
    return offs[:16].T.reshape(-1).astype(np.int64)


def striped8(idx):
    return np.concatenate([x.reshape(-1, 16).T for x in idx]).astype(np.uint16)


def runs(offs, k):
    lists = np.stack([offs[16 * r : 16 * r + 16].T.reshape(-1) for r in range(8)]).astype(np.int64)
    return lists[np.arange(k) % 512 // 64]


def pack_weight(w):
    k, n = w.shape
    w = f64(np.asarray(w, np.float32).astype(ml_dtypes.bfloat16)).reshape(k // 32, 32, n)
    amax = np.abs(w).max(1)
    byte = np.clip(np.where(amax > 0, np.frexp(amax)[1] - 1 + 127 - 7, 1), 1, 254)
    scaled = (w * np.exp2(127.0 - byte)[:, None, :]).reshape(k, n).astype(np.float32)
    words = np.ascontiguousarray(scaled.reshape(k // 512, 128, 4, n).transpose(0, 1, 3, 2)).astype(ml_dtypes.float8_e4m3fn).view(np.uint8)
    return words, np.ascontiguousarray(byte.astype(np.uint8).reshape(k // 512, 16, n))


def unpack_weight(words, scales):
    g, p, n, _ = words.shape
    vals = np.ascontiguousarray(words).view(ml_dtypes.float8_e4m3fn).astype(np.float64) * np.repeat(np.exp2(scales.astype(np.float64) - 127.0), 8, axis=1)[..., None]
    return vals.transpose(0, 1, 3, 2).reshape(g * 512, n)


K, T, S, V, N, G, H = 512, 2048, 512, 256, 512, 2048, 512


def setup_inputs():
    n = np.random.standard_normal
    s = mx_kscale(K)[:, None]
    u = mx_kscale(H)
    packed_xT = pack_weight(n((K, T)) * s)
    packed_dT = pack_weight(n((K, G)) / s)
    perm = np.stack([np.random.permutation(S) for _ in range(8)])
    return {
        "x_words": packed_xT[0],
        "x_scales": packed_xT[1],
        "d_words": packed_dT[0],
        "d_scales": packed_dT[1],
        "gn": (np.random.uniform(0.5, 1.5, (H, 1)) * u[:, None]).astype(np.float32),
        "w1": (n((H, N)) / np.sqrt(H) / u[:, None]).astype(np.float32),
        "offs": striped(np.random.permutation(T)[:S]),
        "kidx": striped8(np.random.randint(0, G, (8, H))),
        "la": striped8(perm[:, :V]),
        "lb": striped8(perm[:, V:]),
    }


def reference(x_words, x_scales, d_words, d_scales, gn, w1, offs, kidx, la, lb):
    d_kidx = unpack_weight(d_words, d_scales)[np.arange(K)[:, None], runs(kidx, K)]
    xq = unpack_weight(x_words, x_scales)[:, unstriped(offs)]
    s = 0.0625 * (d_kidx.T @ xq)
    a = s[np.arange(H)[:, None], runs(la, H)]
    b = s[np.arange(H)[:, None], runs(lb, H)]
    lo = np.minimum(a, b)
    hi = np.maximum(a, b)
    sp = np.zeros((H, S))
    sp[np.arange(H)[:, None], runs(la, H)] = hi
    sd = sp.copy()
    sd[np.arange(H)[:, None], runs(lb, H)] = lo
    z = f64(gn) * sd
    return mxq(f64(w1), 0, "e4m3").T @ mxq(z, 0, "e4m3")

@@ -1,0 +1,199 @@
+from contextlib import ExitStack
+
+import concourse.mybir as mybir
+
+K, T, S, V, N, G, H = 512, 2048, 512, 256, 512, 2048, 512
+FLOPS = 2 * K * H * S + 2 * H * N * S
+
+F32 = mybir.dt.float32
+BF16 = mybir.dt.bfloat16
+I32 = mybir.dt.int32
+U32 = mybir.dt.uint32
+U16 = mybir.dt.uint16
+U8 = mybir.dt.uint8
+FP8X4 = mybir.dt.float8_e4m3fn_x4
+ALU = mybir.AluOpType
+COPY = mybir.ActivationFunctionType.Copy
+
+P = 128
+PACK = 4
+HALF = S // 2
+SCORE_SCALE = 0.0625
+SLOTS = (0, 2, 1, 3)
+
+
+def tile_picked_scoreord_none_p_kernel(
+    tc, x_words, x_scales, d_words, d_scales, gn, w1, offs, kidx, la, lb, out
+):
+    nc = tc.nc
+    with ExitStack() as ctx:
+        keep = ctx.enter_context(tc.tile_pool(name="keep", bufs=1))
+        pairs = ctx.enter_context(tc.tile_pool(name="pairs", bufs=4))
+        windows = ctx.enter_context(tc.tile_pool(name="windows", bufs=2))
+        psum = ctx.enter_context(tc.psum_pool(name="psum", bufs=8))
+
+        offs_t = keep.tile([P, S // 16], U16, name="offs_t")
+        kidx_t = keep.tile([P, H // 16], U16, name="kidx_t")
+        la_t = keep.tile([P, V // 16], U16, name="la_t")
+        lb_t = keep.tile([P, V // 16], U16, name="lb_t")
+        xw = keep.tile([P, T], U32, name="xw", tag="staging", align_bytes=64)
+        dw = keep.tile([P, G], U32, name="dw", align_bytes=64)
+        xs = keep.tile([P, T], U8, name="xs", align_bytes=64)
+        ds = keep.tile([P, G], U8, name="ds", align_bytes=64)
+        ds_mm = keep.tile([P, H], U8, name="ds_mm", align_bytes=64)
+        gn_t = keep.tile([P, PACK], F32, name="gn_t")
+
+        nc.vector.memset(ds[:].bitcast(I32), 0)
+        nc.vector.memset(xs[:].bitcast(I32), 0)
+        nc.vector.memset(ds_mm[:].bitcast(I32), 0)
+
+        nc.sync.dma_start(kidx_t[:], kidx)
+        nc.scalar.dma_start(ds[0:P:8, :].bitcast(I32), d_scales[0].bitcast(I32))
+        nc.sync.dma_start(dw[:].bitcast(I32), d_words[0].rearrange("p n t -> p (n t)").bitcast(I32))
+        nc.sync.dma_start(offs_t[:], offs)
+        for q in range(4):
+            nc.scalar.dma_start(
+                xs[32 * q : 32 * q + 4, :].bitcast(I32), x_scales[0, 4 * q : 4 * q + 4, :].bitcast(I32)
+            )
+        nc.sync.dma_start(xw[:].bitcast(I32), x_words[0].rearrange("p n t -> p (n t)").bitcast(I32))
+        nc.gpsimd.dma_start(gn_t[:], gn.rearrange("(p t) o -> p (t o)", t=PACK))
+        nc.sync.dma_start(la_t[:], la)
+        nc.sync.dma_start(lb_t[:], lb)
+
+        gain = keep.tile([P, PACK], F32, name="gain")
+        nc.scalar.activation(gain[:], gn_t[:], COPY, scale=SCORE_SCALE)
+
+        ds_picked = keep.tile([P, H], U8, name="ds_picked", align_bytes=64)
+        nc.vector.tensor_copy(ds_picked[:], ds[:].indirect(kidx_t[:]))
+        xs_picked = keep.tile([P, S], U8, name="xs_picked", align_bytes=64)
+        ds_dealt = keep.tile([P, H], U8, name="ds_dealt", align_bytes=64)
+        nc.vector.tensor_copy(
+            ds_dealt[:].rearrange("p (t m) -> p t m", t=PACK),
+            ds_picked[:].rearrange("p (m t) -> p t m", t=PACK),
+        )
+        for q in range(4):
+            nc.scalar.dma_start(
+                ds_mm[32 * q : 32 * q + 4, :].bitcast(I32), ds_dealt[32 * q : 32 * q + 32 : 8, :].bitcast(I32)
+            )
+        nc.vector.tensor_copy(xs_picked[:], xs[:].indirect(offs_t[:]))
+
+        dw_picked = keep.tile([P, H], U32, name="dw_picked", align_bytes=64)
+        nc.vector.tensor_copy(dw_picked[:], dw[:].indirect(kidx_t[:]))
+        dw_dealt = keep.tile([P, H], U32, name="dw_dealt", align_bytes=64)
+        nc.vector.tensor_copy(
+            dw_dealt[:].rearrange("p (t c i) -> p c t i", t=PACK, i=4),
+            dw_picked[:].rearrange("p (c i t) -> p c t i", t=PACK, i=4),
+        )
+
+        xw_picked = keep.tile([P, S], U32, name="xw_picked", align_bytes=64)
+        scores = [keep.tile([P, S], F32, name="scores%d" % t, align_bytes=64) for t in range(PACK)]
+
+        def score(t, cols):
+            keys = slice(t * P, (t + 1) * P)
+            width = cols.stop - cols.start
+            bank = psum.tile([P, S], F32, name="bank")
+            nc.tensor.matmul_mx(
+                out=bank[:, 0:width],
+                lhsT=dw_dealt[:, keys].bitcast(FP8X4),
+                lhsT_scale=ds_mm[:, keys],
+                rhs=xw_picked[:, cols].bitcast(FP8X4),
+                rhs_scale=xs_picked[:, cols],
+                start=True,
+                stop=True,
+            )
+            nc.scalar.copy(scores[t][:, cols], bank[:, 0:width])
+
+        for h in range(2):
+            cols = slice(h * HALF, (h + 1) * HALF)
+            nc.vector.tensor_copy(xw_picked[:, cols], xw[:].indirect(offs_t[:, h * 16 : (h + 1) * 16]))
+            score(SLOTS[0], cols)
+        for t in SLOTS[1:]:
+            score(t, slice(0, S))
+
+        w_raw = keep.tile([P, PACK, N], F32, name="w_raw", tag="staging", align_bytes=64)
+        nc.sync.dma_start(w_raw[:], w1.rearrange("(p t) n -> p t n", t=PACK))
+        w_bf = keep.tile([P, N, PACK], BF16, name="w_bf", align_bytes=64)
+        w_codes = keep.tile([P, N], U32, name="w_codes", align_bytes=64)
+        w_sc = keep.tile([P, N], U8, name="w_sc", align_bytes=64)
+        for m in range(4):
+            cols = slice(m * P, (m + 1) * P)
+            nc.scalar.copy(w_bf[:, cols, :], w_raw[:, :, cols].rearrange("p t n -> p n t"))
+
+        def quantise(codes, scales, values, cols):
+            nc.vector.quantize_mx(
+                out=codes[:, cols].bitcast(FP8X4),
+                scales=scales[:, cols],
+                in_=values[:, cols, :].rearrange("p n t -> p (n t)"),
+            )
+
+        z_bf = keep.tile([P, S, PACK], BF16, name="z_bf", align_bytes=64)
+        z_codes = keep.tile([P, S], U32, name="z_codes", align_bytes=64)
+        z_sc = keep.tile([P, S], U8, name="z_sc", align_bytes=64)
+        a, b, hi, lo, sd = {}, {}, {}, {}, {}
+
+        def fetch(dst, u, lst, name):
+            dst[u] = pairs.tile([P, V], F32, name=name)
+            nc.vector.tensor_copy(dst[u][:], scores[SLOTS[u]][:].indirect(lst[:]))
+
+        def order(dst, u, op, name):
+            dst[u] = pairs.tile([P, V], F32, name=name)
+            nc.vector.tensor_tensor(dst[u][:], a[u][:], b[u][:], op)
+
+        def put_hi(u):
+            sd[u] = windows.tile([P, S], F32, name="sd")
+            nc.vector.tensor_copy(sd[u][:].indirect(la_t[:]), hi[u][:])
+
+        def put_lo(u):
+            nc.vector.tensor_copy(sd[u][:].indirect(lb_t[:]), lo[u][:])
+
+        def weigh_scalar(u, cols):
+            t = SLOTS[u]
+            nc.scalar.activation(z_bf[:, cols, t], sd[u][:, cols], COPY, scale=gain[:, t : t + 1])
+
+        for u in (0, 2):
+            fetch(a, u, la_t, "a")
+            fetch(b, u, lb_t, "b")
+            fetch(a, u + 1, la_t, "a")
+            order(hi, u, ALU.max, "hi")
+            fetch(b, u + 1, lb_t, "b")
+            order(lo, u, ALU.min, "lo")
+            put_hi(u)
+            order(hi, u + 1, ALU.max, "hi")
+            put_lo(u)
+            weigh_scalar(u, slice(0, S))
+            order(lo, u + 1, ALU.min, "lo")
+            put_hi(u + 1)
+            quantise(w_codes, w_sc, w_bf, slice(u * P, (u + 2) * P))
+            put_lo(u + 1)
+            if u == 0:
+                weigh_scalar(1, slice(0, S))
+
+        t = SLOTS[3]
+        nc.vector.tensor_scalar(z_bf[:, 0:HALF, t], sd[3][:, 0:HALF], gain[:, t : t + 1], None, ALU.mult)
+        weigh_scalar(3, slice(HALF, S))
+
+        out_v = out.rearrange("(m p) j -> p m j", p=P)
+        for h in range(2):
+            quantise(z_codes, z_sc, z_bf, slice(h * HALF, (h + 1) * HALF))
+        for h in range(2):
+            cols = slice(h * HALF, (h + 1) * HALF)
+            for mp in range(2):
+                staged = pairs.tile([P, 2, HALF], F32, name="staged")
+                for e in range(2):
+                    m = 2 * mp + e
+                    rows = slice(m * P, (m + 1) * P)
+                    bank = psum.tile([P, S], F32, name="bank")
+                    nc.tensor.matmul_mx(
+                        out=bank[:, 0:HALF],
+                        lhsT=w_codes[:, rows].bitcast(FP8X4),
+                        lhsT_scale=w_sc[:, rows],
+                        rhs=z_codes[:, cols].bitcast(FP8X4),
+                        rhs_scale=z_sc[:, cols],
+                        start=True,
+                        stop=True,
+                    )
+                    if e == 0:
+                        nc.scalar.copy(staged[:, e, :], bank[:, 0:HALF])
+                    else:
+                        nc.vector.tensor_copy(staged[:, e, :], bank[:, 0:HALF])
+                nc.sync.dma_start(out_v[:, 2 * mp : 2 * mp + 2, cols], staged[:])

@@ -30,6 +30,7 @@ def tile_picked_scoreord_none_p_kernel(
         keep = ctx.enter_context(tc.tile_pool(name="keep", bufs=1))
         pairs = ctx.enter_context(tc.tile_pool(name="pairs", bufs=4))
         windows = ctx.enter_context(tc.tile_pool(name="windows", bufs=2))
+        stores = ctx.enter_context(tc.tile_pool(name="stores", bufs=8))
         psum = ctx.enter_context(tc.psum_pool(name="psum", bufs=8))
 
         offs_t = keep.tile([P, S // 16], U16, name="offs_t")
@@ -40,44 +41,39 @@ def tile_picked_scoreord_none_p_kernel(
         dw = keep.tile([P, G], U32, name="dw", align_bytes=64)
         xs = keep.tile([P, T], U8, name="xs", align_bytes=64)
         ds = keep.tile([P, G], U8, name="ds", align_bytes=64)
-        ds_mm = keep.tile([P, H], U8, name="ds_mm", align_bytes=64)
+        planes = keep.tile([P, H + S], U8, name="planes", align_bytes=64)
         gn_t = keep.tile([P, PACK], F32, name="gn_t")
 
         nc.vector.memset(ds[:].bitcast(I32), 0)
         nc.vector.memset(xs[:].bitcast(I32), 0)
-        nc.vector.memset(ds_mm[:].bitcast(I32), 0)
+        nc.vector.memset(planes[:].bitcast(I32), 0)
 
         nc.sync.dma_start(kidx_t[:], kidx)
-        nc.scalar.dma_start(ds[0:P:8, :].bitcast(I32), d_scales[0].bitcast(I32))
-        nc.sync.dma_start(dw[:].bitcast(I32), d_words[0].rearrange("p n t -> p (n t)").bitcast(I32))
         nc.sync.dma_start(offs_t[:], offs)
-        for q in range(4):
-            nc.scalar.dma_start(
-                xs[32 * q : 32 * q + 4, :].bitcast(I32), x_scales[0, 4 * q : 4 * q + 4, :].bitcast(I32)
-            )
-        nc.sync.dma_start(xw[:].bitcast(I32), x_words[0].rearrange("p n t -> p (n t)").bitcast(I32))
-        nc.gpsimd.dma_start(gn_t[:], gn.rearrange("(p t) o -> p (t o)", t=PACK))
         nc.sync.dma_start(la_t[:], la)
         nc.sync.dma_start(lb_t[:], lb)
-
-        gain = keep.tile([P, PACK], F32, name="gain")
-        nc.scalar.activation(gain[:], gn_t[:], COPY, scale=SCORE_SCALE)
+        nc.sync.dma_start(ds[0:P:8, :].bitcast(I32), d_scales[0].bitcast(I32))
+        nc.sync.dma_start(xs[0:P:8, :].bitcast(I32), x_scales[0].bitcast(I32))
+        nc.sync.dma_start(dw[:].bitcast(I32), d_words[0].rearrange("p n t -> p (n t)").bitcast(I32))
+        nc.sync.dma_start(xw[:].bitcast(I32), x_words[0].rearrange("p n t -> p (n t)").bitcast(I32))
+        nc.gpsimd.dma_start(gn_t[:], gn.rearrange("(p t) o -> p (t o)", t=PACK))
 
         ds_picked = keep.tile([P, H], U8, name="ds_picked", align_bytes=64)
+        xs_picked = keep.tile([P, S], U8, name="xs_picked", tag="picked", align_bytes=64)
+        spread = keep.tile([P, H + S], U8, name="spread", align_bytes=64)
         nc.vector.tensor_copy(ds_picked[:], ds[:].indirect(kidx_t[:]))
-        xs_picked = keep.tile([P, S], U8, name="xs_picked", align_bytes=64)
-        ds_dealt = keep.tile([P, H], U8, name="ds_dealt", align_bytes=64)
+        nc.vector.tensor_copy(xs_picked[:], xs[:].indirect(offs_t[:]))
         nc.vector.tensor_copy(
-            ds_dealt[:].rearrange("p (t m) -> p t m", t=PACK),
+            spread[:, 0:H].rearrange("p (t m) -> p t m", t=PACK),
             ds_picked[:].rearrange("p (m t) -> p t m", t=PACK),
         )
+        nc.vector.tensor_copy(spread[:, H : H + S].bitcast(I32), xs_picked[:].bitcast(I32))
         for q in range(4):
-            nc.scalar.dma_start(
-                ds_mm[32 * q : 32 * q + 4, :].bitcast(I32), ds_dealt[32 * q : 32 * q + 32 : 8, :].bitcast(I32)
+            nc.sync.dma_start(
+                planes[32 * q : 32 * q + 4, :].bitcast(I32), spread[32 * q : 32 * q + 32 : 8, :].bitcast(I32)
             )
-        nc.vector.tensor_copy(xs_picked[:], xs[:].indirect(offs_t[:]))
 
-        dw_picked = keep.tile([P, H], U32, name="dw_picked", align_bytes=64)
+        dw_picked = keep.tile([P, H], U32, name="dw_picked", tag="picked", align_bytes=64)
         nc.vector.tensor_copy(dw_picked[:], dw[:].indirect(kidx_t[:]))
         dw_dealt = keep.tile([P, H], U32, name="dw_dealt", align_bytes=64)
         nc.vector.tensor_copy(
@@ -85,7 +81,7 @@ def tile_picked_scoreord_none_p_kernel(
             dw_picked[:].rearrange("p (c i t) -> p c t i", t=PACK, i=4),
         )
 
-        xw_picked = keep.tile([P, S], U32, name="xw_picked", align_bytes=64)
+        xw_picked = keep.tile([P, S], U32, name="xw_picked", tag="picked", align_bytes=64)
         scores = [keep.tile([P, S], F32, name="scores%d" % t, align_bytes=64) for t in range(PACK)]
 
         def score(t, cols):
@@ -95,13 +91,13 @@ def tile_picked_scoreord_none_p_kernel(
             nc.tensor.matmul_mx(
                 out=bank[:, 0:width],
                 lhsT=dw_dealt[:, keys].bitcast(FP8X4),
-                lhsT_scale=ds_mm[:, keys],
+                lhsT_scale=planes[:, keys],
                 rhs=xw_picked[:, cols].bitcast(FP8X4),
-                rhs_scale=xs_picked[:, cols],
+                rhs_scale=planes[:, H + cols.start : H + cols.stop],
                 start=True,
                 stop=True,
             )
-            nc.scalar.copy(scores[t][:, cols], bank[:, 0:width])
+            nc.scalar.activation(scores[t][:, cols], bank[:, 0:width], COPY, scale=SCORE_SCALE)
 
         for h in range(2):
             cols = slice(h * HALF, (h + 1) * HALF)
@@ -148,7 +144,7 @@ def tile_picked_scoreord_none_p_kernel(
 
         def weigh_scalar(u, cols):
             t = SLOTS[u]
-            nc.scalar.activation(z_bf[:, cols, t], sd[u][:, cols], COPY, scale=gain[:, t : t + 1])
+            nc.scalar.activation(z_bf[:, cols, t], sd[u][:, cols], COPY, scale=gn_t[:, t : t + 1])
 
         for u in (0, 2):
             fetch(a, u, la_t, "a")
@@ -169,31 +165,28 @@ def tile_picked_scoreord_none_p_kernel(
                 weigh_scalar(1, slice(0, S))
 
         t = SLOTS[3]
-        nc.vector.tensor_scalar(z_bf[:, 0:HALF, t], sd[3][:, 0:HALF], gain[:, t : t + 1], None, ALU.mult)
+        nc.vector.tensor_scalar(z_bf[:, 0:HALF, t], sd[3][:, 0:HALF], gn_t[:, t : t + 1], None, ALU.mult)
         weigh_scalar(3, slice(HALF, S))
 
-        out_v = out.rearrange("(m p) j -> p m j", p=P)
         for h in range(2):
             quantise(z_codes, z_sc, z_bf, slice(h * HALF, (h + 1) * HALF))
         for h in range(2):
             cols = slice(h * HALF, (h + 1) * HALF)
-            for mp in range(2):
-                staged = pairs.tile([P, 2, HALF], F32, name="staged")
-                for e in range(2):
-                    m = 2 * mp + e
-                    rows = slice(m * P, (m + 1) * P)
-                    bank = psum.tile([P, S], F32, name="bank")
-                    nc.tensor.matmul_mx(
-                        out=bank[:, 0:HALF],
-                        lhsT=w_codes[:, rows].bitcast(FP8X4),
-                        lhsT_scale=w_sc[:, rows],
-                        rhs=z_codes[:, cols].bitcast(FP8X4),
-                        rhs_scale=z_sc[:, cols],
-                        start=True,
-                        stop=True,
-                    )
-                    if e == 0:
-                        nc.scalar.copy(staged[:, e, :], bank[:, 0:HALF])
-                    else:
-                        nc.vector.tensor_copy(staged[:, e, :], bank[:, 0:HALF])
-                nc.sync.dma_start(out_v[:, 2 * mp : 2 * mp + 2, cols], staged[:])
+            for m in range(4):
+                rows = slice(m * P, (m + 1) * P)
+                bank = psum.tile([P, S], F32, name="bank")
+                nc.tensor.matmul_mx(
+                    out=bank[:, 0:HALF],
+                    lhsT=w_codes[:, rows].bitcast(FP8X4),
+                    lhsT_scale=w_sc[:, rows],
+                    rhs=z_codes[:, cols].bitcast(FP8X4),
+                    rhs_scale=z_sc[:, cols],
+                    start=True,
+                    stop=True,
+                )
+                staged = stores.tile([P, HALF], F32, name="staged")
+                if m % 2 == 0:
+                    nc.scalar.copy(staged[:], bank[:, 0:HALF])
+                else:
+                    nc.vector.tensor_copy(staged[:], bank[:, 0:HALF])
+                nc.sync.dma_start(out[rows, cols], staged[:])

@@ -42,7 +42,6 @@ def tile_picked_scoreord_none_p_kernel(
         xs = keep.tile([P, T], U8, name="xs", align_bytes=64)
         ds = keep.tile([P, G], U8, name="ds", align_bytes=64)
         planes = keep.tile([P, H + S], U8, name="planes", align_bytes=64)
-        gn_t = keep.tile([P, PACK], F32, name="gn_t")
 
         nc.vector.memset(ds[:].bitcast(I32), 0)
         nc.vector.memset(xs[:].bitcast(I32), 0)
@@ -50,22 +49,21 @@ def tile_picked_scoreord_none_p_kernel(
 
         nc.sync.dma_start(kidx_t[:], kidx)
         nc.sync.dma_start(offs_t[:], offs)
-        nc.sync.dma_start(la_t[:], la)
-        nc.sync.dma_start(lb_t[:], lb)
-        nc.sync.dma_start(ds[0:P:8, :].bitcast(I32), d_scales[0].bitcast(I32))
-        nc.sync.dma_start(xs[0:P:8, :].bitcast(I32), x_scales[0].bitcast(I32))
+        nc.scalar.dma_start(ds[0:P:8, :].bitcast(I32), d_scales[0].bitcast(I32))
+        nc.scalar.dma_start(xs[0:P:8, :].bitcast(I32), x_scales[0].bitcast(I32))
         nc.sync.dma_start(dw[:].bitcast(I32), d_words[0].rearrange("p n t -> p (n t)").bitcast(I32))
+        nc.sync.dma_start(la_t[:], la)
         nc.sync.dma_start(xw[:].bitcast(I32), x_words[0].rearrange("p n t -> p (n t)").bitcast(I32))
-        nc.gpsimd.dma_start(gn_t[:], gn.rearrange("(p t) o -> p (t o)", t=PACK))
+        nc.sync.dma_start(lb_t[:], lb)
 
         ds_picked = keep.tile([P, H], U8, name="ds_picked", align_bytes=64)
-        xs_picked = keep.tile([P, S], U8, name="xs_picked", tag="picked", align_bytes=64)
+        xs_picked = keep.tile([P, S], U8, name="xs_picked", align_bytes=64)
         spread = keep.tile([P, H + S], U8, name="spread", align_bytes=64)
         nc.vector.tensor_copy(ds_picked[:], ds[:].indirect(kidx_t[:]))
         nc.vector.tensor_copy(xs_picked[:], xs[:].indirect(offs_t[:]))
         nc.vector.tensor_copy(
-            spread[:, 0:H].rearrange("p (t m) -> p t m", t=PACK),
-            ds_picked[:].rearrange("p (m t) -> p t m", t=PACK),
+            spread[:, 0:H].bitcast(I32).rearrange("p (t g w) -> p t g w", t=PACK, w=2),
+            ds_picked[:].bitcast(I32).rearrange("p (g t w) -> p t g w", t=PACK, w=2),
         )
         nc.vector.tensor_copy(spread[:, H : H + S].bitcast(I32), xs_picked[:].bitcast(I32))
         for q in range(4):
@@ -76,12 +74,14 @@ def tile_picked_scoreord_none_p_kernel(
         dw_picked = keep.tile([P, H], U32, name="dw_picked", tag="picked", align_bytes=64)
         nc.vector.tensor_copy(dw_picked[:], dw[:].indirect(kidx_t[:]))
         dw_dealt = keep.tile([P, H], U32, name="dw_dealt", align_bytes=64)
-        nc.vector.tensor_copy(
-            dw_dealt[:].rearrange("p (t c i) -> p c t i", t=PACK, i=4),
-            dw_picked[:].rearrange("p (c i t) -> p c t i", t=PACK, i=4),
-        )
 
-        xw_picked = keep.tile([P, S], U32, name="xw_picked", tag="picked", align_bytes=64)
+        def deal_words(t):
+            nc.vector.tensor_copy(
+                dw_dealt[:, t * P : (t + 1) * P].rearrange("p (g q) -> p g q", q=8),
+                dw_picked[:].rearrange("p (g t q) -> p t g q", t=PACK, q=8)[:, t, :, :],
+            )
+
+        xw_picked = keep.tile([P, S], U32, name="xw_picked", align_bytes=64)
         scores = [keep.tile([P, S], F32, name="scores%d" % t, align_bytes=64) for t in range(PACK)]
 
         def score(t, cols):
@@ -99,15 +99,25 @@ def tile_picked_scoreord_none_p_kernel(
             )
             nc.scalar.activation(scores[t][:, cols], bank[:, 0:width], COPY, scale=SCORE_SCALE)
 
-        for h in range(2):
-            cols = slice(h * HALF, (h + 1) * HALF)
-            nc.vector.tensor_copy(xw_picked[:, cols], xw[:].indirect(offs_t[:, h * 16 : (h + 1) * 16]))
-            score(SLOTS[0], cols)
+        halves = [slice(h * HALF, (h + 1) * HALF) for h in range(2)]
+        nc.vector.tensor_copy(xw_picked[:, halves[0]], xw[:].indirect(offs_t[:, 0:16]))
+        deal_words(SLOTS[0])
+        score(SLOTS[0], halves[0])
+        nc.vector.tensor_copy(xw_picked[:, halves[1]], xw[:].indirect(offs_t[:, 16:32]))
+        score(SLOTS[0], halves[1])
         for t in SLOTS[1:]:
+            deal_words(t)
             score(t, slice(0, S))
 
         w_raw = keep.tile([P, PACK, N], F32, name="w_raw", tag="staging", align_bytes=64)
-        nc.sync.dma_start(w_raw[:], w1.rearrange("(p t) n -> p t n", t=PACK))
+        gn_t = keep.tile([P, PACK], F32, name="gn_t", tag="picked", align_bytes=64)
+        w_rows = w1.rearrange("(g t q) n -> q g t n", t=PACK, q=8)
+        gn_rows = gn.rearrange("(g t q) o -> q g (t o)", t=PACK, q=8)
+        for q in range(8):
+            nc.sync.dma_start(w_raw[q:P:8, :, :], w_rows[q])
+        with nc.allow_non_contiguous_dma(reason="one weight a key"):
+            for q in range(8):
+                nc.sync.dma_start(gn_t[q:P:8, :], gn_rows[q])
         w_bf = keep.tile([P, N, PACK], BF16, name="w_bf", align_bytes=64)
         w_codes = keep.tile([P, N], U32, name="w_codes", align_bytes=64)
         w_sc = keep.tile([P, N], U8, name="w_sc", align_bytes=64)
@@ -122,7 +132,7 @@ def tile_picked_scoreord_none_p_kernel(
                 in_=values[:, cols, :].rearrange("p n t -> p (n t)"),
             )
 
-        z_bf = keep.tile([P, S, PACK], BF16, name="z_bf", align_bytes=64)
+        z_bf = keep.tile([P, S, PACK], BF16, name="z_bf", tag="staging", align_bytes=64)
         z_codes = keep.tile([P, S], U32, name="z_codes", align_bytes=64)
         z_sc = keep.tile([P, S], U8, name="z_sc", align_bytes=64)
         a, b, hi, lo, sd = {}, {}, {}, {}, {}
@@ -153,16 +163,16 @@ def tile_picked_scoreord_none_p_kernel(
             order(hi, u, ALU.max, "hi")
             fetch(b, u + 1, lb_t, "b")
             order(lo, u, ALU.min, "lo")
-            put_hi(u)
             order(hi, u + 1, ALU.max, "hi")
+            order(lo, u + 1, ALU.min, "lo")
+            put_hi(u)
+            put_hi(u + 1)
             put_lo(u)
             weigh_scalar(u, slice(0, S))
-            order(lo, u + 1, ALU.min, "lo")
-            put_hi(u + 1)
-            quantise(w_codes, w_sc, w_bf, slice(u * P, (u + 2) * P))
             put_lo(u + 1)
             if u == 0:
                 weigh_scalar(1, slice(0, S))
+                quantise(w_codes, w_sc, w_bf, slice(0, N))
 
         t = SLOTS[3]
         nc.vector.tensor_scalar(z_bf[:, 0:HALF, t], sd[3][:, 0:HALF], gn_t[:, t : t + 1], None, ALU.mult)

@@ -17,9 +17,16 @@ COPY = mybir.ActivationFunctionType.Copy
 
 P = 128
 PACK = 4
+BLOCK_ROWS = 8
+QUADRANT = 32
+GROUP = 16
 HALF = S // 2
+HALVES = (slice(0, HALF), slice(HALF, S))
+ALL_QUERIES = slice(0, S)
 SCORE_SCALE = 0.0625
-SLOTS = (0, 2, 1, 3)
+TILE_PAIRS = ((0, 2), (1, 3))
+FIRST_TILE = TILE_PAIRS[0][0]
+LAST_TILE = TILE_PAIRS[-1][-1]
 
 
 def tile_picked_scoreord_none_p_kernel(
@@ -28,17 +35,17 @@ def tile_picked_scoreord_none_p_kernel(
     nc = tc.nc
     with ExitStack() as ctx:
         keep = ctx.enter_context(tc.tile_pool(name="keep", bufs=1))
-        pairs = ctx.enter_context(tc.tile_pool(name="pairs", bufs=4))
+        pairs = ctx.enter_context(tc.tile_pool(name="pairs", bufs=PACK))
         windows = ctx.enter_context(tc.tile_pool(name="windows", bufs=2))
         stores = ctx.enter_context(tc.tile_pool(name="stores", bufs=8))
         psum = ctx.enter_context(tc.psum_pool(name="psum", bufs=8))
 
-        offs_t = keep.tile([P, S // 16], U16, name="offs_t")
-        kidx_t = keep.tile([P, H // 16], U16, name="kidx_t")
-        la_t = keep.tile([P, V // 16], U16, name="la_t")
-        lb_t = keep.tile([P, V // 16], U16, name="lb_t")
-        xw = keep.tile([P, T], U32, name="xw", tag="staging", align_bytes=64)
-        dw = keep.tile([P, G], U32, name="dw", align_bytes=64)
+        offs_t = keep.tile([P, S // GROUP], U16, name="offs_t")
+        kidx_t = keep.tile([P, H // GROUP], U16, name="kidx_t")
+        la_t = keep.tile([P, V // GROUP], U16, name="la_t")
+        lb_t = keep.tile([P, V // GROUP], U16, name="lb_t")
+        xw = keep.tile([P, T], U32, name="xw", tag="x_space", align_bytes=64)
+        dw = keep.tile([P, G], U32, name="dw", tag="d_space", align_bytes=64)
         xs = keep.tile([P, T], U8, name="xs", align_bytes=64)
         ds = keep.tile([P, G], U8, name="ds", align_bytes=64)
         planes = keep.tile([P, H + S], U8, name="planes", align_bytes=64)
@@ -49,12 +56,12 @@ def tile_picked_scoreord_none_p_kernel(
 
         nc.sync.dma_start(kidx_t[:], kidx)
         nc.sync.dma_start(offs_t[:], offs)
-        nc.scalar.dma_start(ds[0:P:8, :].bitcast(I32), d_scales[0].bitcast(I32))
-        nc.scalar.dma_start(xs[0:P:8, :].bitcast(I32), x_scales[0].bitcast(I32))
-        nc.sync.dma_start(dw[:].bitcast(I32), d_words[0].rearrange("p n t -> p (n t)").bitcast(I32))
         nc.sync.dma_start(la_t[:], la)
-        nc.sync.dma_start(xw[:].bitcast(I32), x_words[0].rearrange("p n t -> p (n t)").bitcast(I32))
         nc.sync.dma_start(lb_t[:], lb)
+        nc.sync.dma_start(ds[0:P:BLOCK_ROWS, :].bitcast(I32), d_scales[0].bitcast(I32))
+        nc.sync.dma_start(xs[0:P:BLOCK_ROWS, :].bitcast(I32), x_scales[0].bitcast(I32))
+        nc.sync.dma_start(dw[:].bitcast(I32), d_words[0].rearrange("p n t -> p (n t)").bitcast(I32))
+        nc.sync.dma_start(xw[:].bitcast(I32), x_words[0].rearrange("p n t -> p (n t)").bitcast(I32))
 
         ds_picked = keep.tile([P, H], U8, name="ds_picked", align_bytes=64)
         xs_picked = keep.tile([P, S], U8, name="xs_picked", align_bytes=64)
@@ -66,23 +73,28 @@ def tile_picked_scoreord_none_p_kernel(
             ds_picked[:].bitcast(I32).rearrange("p (g t w) -> p t g w", t=PACK, w=2),
         )
         nc.vector.tensor_copy(spread[:, H : H + S].bitcast(I32), xs_picked[:].bitcast(I32))
-        for q in range(4):
+        for first in range(0, P, QUADRANT):
             nc.sync.dma_start(
-                planes[32 * q : 32 * q + 4, :].bitcast(I32), spread[32 * q : 32 * q + 32 : 8, :].bitcast(I32)
+                planes[first : first + QUADRANT // BLOCK_ROWS, :].bitcast(I32),
+                spread[first : first + QUADRANT : BLOCK_ROWS, :].bitcast(I32),
             )
 
-        dw_picked = keep.tile([P, H], U32, name="dw_picked", tag="picked", align_bytes=64)
+        dw_picked = keep.tile([P, H], U32, name="dw_picked", align_bytes=64)
         nc.vector.tensor_copy(dw_picked[:], dw[:].indirect(kidx_t[:]))
         dw_dealt = keep.tile([P, H], U32, name="dw_dealt", align_bytes=64)
+        xw_picked = keep.tile([P, S], U32, name="xw_picked", align_bytes=64)
+        scores = [keep.tile([P, S], F32, name="scores%d" % t, align_bytes=64) for t in range(PACK)]
 
         def deal_words(t):
             nc.vector.tensor_copy(
-                dw_dealt[:, t * P : (t + 1) * P].rearrange("p (g q) -> p g q", q=8),
-                dw_picked[:].rearrange("p (g t q) -> p t g q", t=PACK, q=8)[:, t, :, :],
+                dw_dealt[:, t * P : (t + 1) * P].rearrange("p (g q) -> p g q", q=BLOCK_ROWS),
+                dw_picked[:].rearrange("p (g t q) -> p t g q", t=PACK, q=BLOCK_ROWS)[:, t, :, :],
             )
 
-        xw_picked = keep.tile([P, S], U32, name="xw_picked", align_bytes=64)
-        scores = [keep.tile([P, S], F32, name="scores%d" % t, align_bytes=64) for t in range(PACK)]
+        def pick_queries(cols):
+            nc.vector.tensor_copy(
+                xw_picked[:, cols], xw[:].indirect(offs_t[:, cols.start // GROUP : cols.stop // GROUP])
+            )
 
         def score(t, cols):
             keys = slice(t * P, (t + 1) * P)
@@ -99,29 +111,29 @@ def tile_picked_scoreord_none_p_kernel(
             )
             nc.scalar.activation(scores[t][:, cols], bank[:, 0:width], COPY, scale=SCORE_SCALE)
 
-        halves = [slice(h * HALF, (h + 1) * HALF) for h in range(2)]
-        nc.vector.tensor_copy(xw_picked[:, halves[0]], xw[:].indirect(offs_t[:, 0:16]))
-        deal_words(SLOTS[0])
-        score(SLOTS[0], halves[0])
-        nc.vector.tensor_copy(xw_picked[:, halves[1]], xw[:].indirect(offs_t[:, 16:32]))
-        score(SLOTS[0], halves[1])
-        for t in SLOTS[1:]:
+        pick_queries(HALVES[0])
+        deal_words(FIRST_TILE)
+        score(FIRST_TILE, HALVES[0])
+        pick_queries(HALVES[1])
+        score(FIRST_TILE, HALVES[1])
+        for t in [t for pair in TILE_PAIRS for t in pair][1:]:
             deal_words(t)
-            score(t, slice(0, S))
+            score(t, ALL_QUERIES)
 
-        w_raw = keep.tile([P, PACK, N], F32, name="w_raw", tag="staging", align_bytes=64)
-        gn_t = keep.tile([P, PACK], F32, name="gn_t", tag="picked", align_bytes=64)
-        w_rows = w1.rearrange("(g t q) n -> q g t n", t=PACK, q=8)
-        gn_rows = gn.rearrange("(g t q) o -> q g (t o)", t=PACK, q=8)
-        for q in range(8):
-            nc.sync.dma_start(w_raw[q:P:8, :, :], w_rows[q])
-        with nc.allow_non_contiguous_dma(reason="one weight a key"):
-            for q in range(8):
-                nc.sync.dma_start(gn_t[q:P:8, :], gn_rows[q])
+        w_raw = keep.tile([P, PACK, N], F32, name="w_raw", tag="d_space", align_bytes=64)
+        gn_t = keep.tile([P, PACK], F32, name="gn_t", tag="x_space", align_bytes=64)
+        w_rows = w1.rearrange("(g t q) n -> q g t n", t=PACK, q=BLOCK_ROWS)
+        gn_rows = gn.rearrange("(g t q) o -> q g (t o)", t=PACK, q=BLOCK_ROWS)
+        for q in range(BLOCK_ROWS):
+            nc.sync.dma_start(w_raw[q:P:BLOCK_ROWS, :, :], w_rows[q])
+        with nc.allow_non_contiguous_dma(reason="one weight a key, eight keys apart"):
+            for q in range(BLOCK_ROWS):
+                nc.sync.dma_start(gn_t[q:P:BLOCK_ROWS, :], gn_rows[q])
+
         w_bf = keep.tile([P, N, PACK], BF16, name="w_bf", align_bytes=64)
         w_codes = keep.tile([P, N], U32, name="w_codes", align_bytes=64)
         w_sc = keep.tile([P, N], U8, name="w_sc", align_bytes=64)
-        for m in range(4):
+        for m in range(N // P):
             cols = slice(m * P, (m + 1) * P)
             nc.scalar.copy(w_bf[:, cols, :], w_raw[:, :, cols].rearrange("p t n -> p n t"))
 
@@ -132,57 +144,55 @@ def tile_picked_scoreord_none_p_kernel(
                 in_=values[:, cols, :].rearrange("p n t -> p (n t)"),
             )
 
-        z_bf = keep.tile([P, S, PACK], BF16, name="z_bf", tag="staging", align_bytes=64)
+        z_bf = keep.tile([P, S, PACK], BF16, name="z_bf", tag="d_space", align_bytes=64)
         z_codes = keep.tile([P, S], U32, name="z_codes", align_bytes=64)
         z_sc = keep.tile([P, S], U8, name="z_sc", align_bytes=64)
         a, b, hi, lo, sd = {}, {}, {}, {}, {}
 
-        def fetch(dst, u, lst, name):
-            dst[u] = pairs.tile([P, V], F32, name=name)
-            nc.vector.tensor_copy(dst[u][:], scores[SLOTS[u]][:].indirect(lst[:]))
+        def fetch(fetched, t, places, name):
+            fetched[t] = pairs.tile([P, V], F32, name=name)
+            nc.vector.tensor_copy(fetched[t][:], scores[t][:].indirect(places[:]))
 
-        def order(dst, u, op, name):
-            dst[u] = pairs.tile([P, V], F32, name=name)
-            nc.vector.tensor_tensor(dst[u][:], a[u][:], b[u][:], op)
+        def compare(chosen, t, op, name):
+            chosen[t] = pairs.tile([P, V], F32, name=name)
+            nc.vector.tensor_tensor(chosen[t][:], a[t][:], b[t][:], op)
 
-        def put_hi(u):
-            sd[u] = windows.tile([P, S], F32, name="sd")
-            nc.vector.tensor_copy(sd[u][:].indirect(la_t[:]), hi[u][:])
+        def put_hi(t):
+            sd[t] = windows.tile([P, S], F32, name="sd")
+            nc.vector.tensor_copy(sd[t][:].indirect(la_t[:]), hi[t][:])
 
-        def put_lo(u):
-            nc.vector.tensor_copy(sd[u][:].indirect(lb_t[:]), lo[u][:])
+        def put_lo(t):
+            nc.vector.tensor_copy(sd[t][:].indirect(lb_t[:]), lo[t][:])
 
-        def weigh_scalar(u, cols):
-            t = SLOTS[u]
-            nc.scalar.activation(z_bf[:, cols, t], sd[u][:, cols], COPY, scale=gn_t[:, t : t + 1])
+        def weigh_on_scalar(t, cols):
+            nc.scalar.activation(z_bf[:, cols, t], sd[t][:, cols], COPY, scale=gn_t[:, t : t + 1])
 
-        for u in (0, 2):
-            fetch(a, u, la_t, "a")
-            fetch(b, u, lb_t, "b")
-            fetch(a, u + 1, la_t, "a")
-            order(hi, u, ALU.max, "hi")
-            fetch(b, u + 1, lb_t, "b")
-            order(lo, u, ALU.min, "lo")
-            order(hi, u + 1, ALU.max, "hi")
-            order(lo, u + 1, ALU.min, "lo")
-            put_hi(u)
-            put_hi(u + 1)
-            put_lo(u)
-            weigh_scalar(u, slice(0, S))
-            put_lo(u + 1)
-            if u == 0:
-                weigh_scalar(1, slice(0, S))
-                quantise(w_codes, w_sc, w_bf, slice(0, N))
+        for turn, (t0, t1) in enumerate(TILE_PAIRS):
+            fetch(a, t0, la_t, "a")
+            fetch(b, t0, lb_t, "b")
+            fetch(a, t1, la_t, "a")
+            compare(hi, t0, ALU.max, "hi")
+            fetch(b, t1, lb_t, "b")
+            compare(lo, t0, ALU.min, "lo")
+            put_hi(t0)
+            compare(hi, t1, ALU.max, "hi")
+            put_lo(t0)
+            weigh_on_scalar(t0, ALL_QUERIES)
+            compare(lo, t1, ALU.min, "lo")
+            put_hi(t1)
+            quantise(w_codes, w_sc, w_bf, slice(turn * N // 2, (turn + 1) * N // 2))
+            put_lo(t1)
+            if t1 != LAST_TILE:
+                weigh_on_scalar(t1, ALL_QUERIES)
 
-        t = SLOTS[3]
-        nc.vector.tensor_scalar(z_bf[:, 0:HALF, t], sd[3][:, 0:HALF], gn_t[:, t : t + 1], None, ALU.mult)
-        weigh_scalar(3, slice(HALF, S))
+        gn_last = gn_t[:, LAST_TILE : LAST_TILE + 1]
+        nc.vector.tensor_scalar(z_bf[:, HALVES[0], LAST_TILE], sd[LAST_TILE][:, HALVES[0]], gn_last, None, ALU.mult)
+        weigh_on_scalar(LAST_TILE, HALVES[1])
 
-        for h in range(2):
-            quantise(z_codes, z_sc, z_bf, slice(h * HALF, (h + 1) * HALF))
-        for h in range(2):
-            cols = slice(h * HALF, (h + 1) * HALF)
-            for m in range(4):
+        for cols in HALVES:
+            quantise(z_codes, z_sc, z_bf, cols)
+        for cols in HALVES:
+            for m in range(N // P):
                 rows = slice(m * P, (m + 1) * P)
                 bank = psum.tile([P, S], F32, name="bank")
                 nc.tensor.matmul_mx(

from contextlib import ExitStack

import concourse.mybir as mybir

K, T, S, V, N, G, H = 512, 2048, 512, 256, 512, 2048, 512
FLOPS = 2 * K * H * S + 2 * H * N * S

F32 = mybir.dt.float32
BF16 = mybir.dt.bfloat16
I32 = mybir.dt.int32
U32 = mybir.dt.uint32
U16 = mybir.dt.uint16
U8 = mybir.dt.uint8
FP8X4 = mybir.dt.float8_e4m3fn_x4
ALU = mybir.AluOpType
COPY = mybir.ActivationFunctionType.Copy

P = 128
PACK = 4
BLOCK_ROWS = 8
QUADRANT = 32
GROUP = 16
HALF = S // 2
HALVES = (slice(0, HALF), slice(HALF, S))
ALL_QUERIES = slice(0, S)
SCORE_SCALE = 0.0625
TILE_PAIRS = ((0, 2), (1, 3))
FIRST_TILE = TILE_PAIRS[0][0]
LAST_TILE = TILE_PAIRS[-1][-1]


def tile_picked_scoreord_none_p_kernel(
    tc, x_words, x_scales, d_words, d_scales, gn, w1, offs, kidx, la, lb, out
):
    nc = tc.nc
    with ExitStack() as ctx:
        keep = ctx.enter_context(tc.tile_pool(name="keep", bufs=1))
        pairs = ctx.enter_context(tc.tile_pool(name="pairs", bufs=PACK))
        windows = ctx.enter_context(tc.tile_pool(name="windows", bufs=2))
        stores = ctx.enter_context(tc.tile_pool(name="stores", bufs=8))
        psum = ctx.enter_context(tc.psum_pool(name="psum", bufs=8))

        offs_t = keep.tile([P, S // GROUP], U16, name="offs_t")
        kidx_t = keep.tile([P, H // GROUP], U16, name="kidx_t")
        la_t = keep.tile([P, V // GROUP], U16, name="la_t")
        lb_t = keep.tile([P, V // GROUP], U16, name="lb_t")
        xw = keep.tile([P, T], U32, name="xw", tag="x_space", align_bytes=64)
        dw = keep.tile([P, G], U32, name="dw", tag="d_space", align_bytes=64)
        xs = keep.tile([P, T], U8, name="xs", align_bytes=64)
        ds = keep.tile([P, G], U8, name="ds", align_bytes=64)
        planes = keep.tile([P, H + S], U8, name="planes", align_bytes=64)

        nc.vector.memset(ds[:].bitcast(I32), 0)
        nc.vector.memset(xs[:].bitcast(I32), 0)
        nc.vector.memset(planes[:].bitcast(I32), 0)

        nc.sync.dma_start(kidx_t[:], kidx)
        nc.sync.dma_start(offs_t[:], offs)
        nc.sync.dma_start(la_t[:], la)
        nc.sync.dma_start(lb_t[:], lb)
        nc.sync.dma_start(ds[0:P:BLOCK_ROWS, :].bitcast(I32), d_scales[0].bitcast(I32))
        nc.sync.dma_start(xs[0:P:BLOCK_ROWS, :].bitcast(I32), x_scales[0].bitcast(I32))
        nc.sync.dma_start(dw[:].bitcast(I32), d_words[0].rearrange("p n t -> p (n t)").bitcast(I32))
        nc.sync.dma_start(xw[:].bitcast(I32), x_words[0].rearrange("p n t -> p (n t)").bitcast(I32))

        ds_picked = keep.tile([P, H], U8, name="ds_picked", align_bytes=64)
        xs_picked = keep.tile([P, S], U8, name="xs_picked", align_bytes=64)
        spread = keep.tile([P, H + S], U8, name="spread", align_bytes=64)
        nc.vector.tensor_copy(ds_picked[:], ds[:].indirect(kidx_t[:]))
        nc.vector.tensor_copy(xs_picked[:], xs[:].indirect(offs_t[:]))
        nc.vector.tensor_copy(
            spread[:, 0:H].bitcast(I32).rearrange("p (t g w) -> p t g w", t=PACK, w=2),
            ds_picked[:].bitcast(I32).rearrange("p (g t w) -> p t g w", t=PACK, w=2),
        )
        nc.vector.tensor_copy(spread[:, H : H + S].bitcast(I32), xs_picked[:].bitcast(I32))
        for first in range(0, P, QUADRANT):
            nc.sync.dma_start(
                planes[first : first + QUADRANT // BLOCK_ROWS, :].bitcast(I32),
                spread[first : first + QUADRANT : BLOCK_ROWS, :].bitcast(I32),
            )

        dw_picked = keep.tile([P, H], U32, name="dw_picked", align_bytes=64)
        nc.vector.tensor_copy(dw_picked[:], dw[:].indirect(kidx_t[:]))
        dw_dealt = keep.tile([P, H], U32, name="dw_dealt", align_bytes=64)
        xw_picked = keep.tile([P, S], U32, name="xw_picked", align_bytes=64)
        scores = [keep.tile([P, S], F32, name="scores%d" % t, align_bytes=64) for t in range(PACK)]

        def deal_words(t):
            nc.vector.tensor_copy(
                dw_dealt[:, t * P : (t + 1) * P].rearrange("p (g q) -> p g q", q=BLOCK_ROWS),
                dw_picked[:].rearrange("p (g t q) -> p t g q", t=PACK, q=BLOCK_ROWS)[:, t, :, :],
            )

        def pick_queries(cols):
            nc.vector.tensor_copy(
                xw_picked[:, cols], xw[:].indirect(offs_t[:, cols.start // GROUP : cols.stop // GROUP])
            )

        def score(t, cols):
            keys = slice(t * P, (t + 1) * P)
            width = cols.stop - cols.start
            bank = psum.tile([P, S], F32, name="bank")
            nc.tensor.matmul_mx(
                out=bank[:, 0:width],
                lhsT=dw_dealt[:, keys].bitcast(FP8X4),
                lhsT_scale=planes[:, keys],
                rhs=xw_picked[:, cols].bitcast(FP8X4),
                rhs_scale=planes[:, H + cols.start : H + cols.stop],
                start=True,
                stop=True,
            )
            nc.scalar.activation(scores[t][:, cols], bank[:, 0:width], COPY, scale=SCORE_SCALE)

        pick_queries(HALVES[0])
        deal_words(FIRST_TILE)
        score(FIRST_TILE, HALVES[0])
        pick_queries(HALVES[1])
        score(FIRST_TILE, HALVES[1])
        for t in [t for pair in TILE_PAIRS for t in pair][1:]:
            deal_words(t)
            score(t, ALL_QUERIES)

        w_raw = keep.tile([P, PACK, N], F32, name="w_raw", tag="d_space", align_bytes=64)
        gn_t = keep.tile([P, PACK], F32, name="gn_t", tag="x_space", align_bytes=64)
        w_rows = w1.rearrange("(g t q) n -> q g t n", t=PACK, q=BLOCK_ROWS)
        gn_rows = gn.rearrange("(g t q) o -> q g (t o)", t=PACK, q=BLOCK_ROWS)
        for q in range(BLOCK_ROWS):
            nc.sync.dma_start(w_raw[q:P:BLOCK_ROWS, :, :], w_rows[q])
        with nc.allow_non_contiguous_dma(reason="one weight a key, eight keys apart"):
            for q in range(BLOCK_ROWS):
                nc.sync.dma_start(gn_t[q:P:BLOCK_ROWS, :], gn_rows[q])

        w_bf = keep.tile([P, N, PACK], BF16, name="w_bf", align_bytes=64)
        w_codes = keep.tile([P, N], U32, name="w_codes", align_bytes=64)
        w_sc = keep.tile([P, N], U8, name="w_sc", align_bytes=64)
        for m in range(N // P):
            cols = slice(m * P, (m + 1) * P)
            nc.scalar.copy(w_bf[:, cols, :], w_raw[:, :, cols].rearrange("p t n -> p n t"))

        def quantise(codes, scales, values, cols):
            nc.vector.quantize_mx(
                out=codes[:, cols].bitcast(FP8X4),
                scales=scales[:, cols],
                in_=values[:, cols, :].rearrange("p n t -> p (n t)"),
            )

        z_bf = keep.tile([P, S, PACK], BF16, name="z_bf", tag="d_space", align_bytes=64)
        z_codes = keep.tile([P, S], U32, name="z_codes", align_bytes=64)
        z_sc = keep.tile([P, S], U8, name="z_sc", align_bytes=64)
        a, b, hi, lo, sd = {}, {}, {}, {}, {}

        def fetch(fetched, t, places, name):
            fetched[t] = pairs.tile([P, V], F32, name=name)
            nc.vector.tensor_copy(fetched[t][:], scores[t][:].indirect(places[:]))

        def compare(chosen, t, op, name):
            chosen[t] = pairs.tile([P, V], F32, name=name)
            nc.vector.tensor_tensor(chosen[t][:], a[t][:], b[t][:], op)

        def put_hi(t):
            sd[t] = windows.tile([P, S], F32, name="sd")
            nc.vector.tensor_copy(sd[t][:].indirect(la_t[:]), hi[t][:])

        def put_lo(t):
            nc.vector.tensor_copy(sd[t][:].indirect(lb_t[:]), lo[t][:])

        def weigh_on_scalar(t, cols):
            nc.scalar.activation(z_bf[:, cols, t], sd[t][:, cols], COPY, scale=gn_t[:, t : t + 1])

        for turn, (t0, t1) in enumerate(TILE_PAIRS):
            fetch(a, t0, la_t, "a")
            fetch(b, t0, lb_t, "b")
            fetch(a, t1, la_t, "a")
            compare(hi, t0, ALU.max, "hi")
            fetch(b, t1, lb_t, "b")
            compare(lo, t0, ALU.min, "lo")
            put_hi(t0)
            compare(hi, t1, ALU.max, "hi")
            put_lo(t0)
            weigh_on_scalar(t0, ALL_QUERIES)
            compare(lo, t1, ALU.min, "lo")
            put_hi(t1)
            quantise(w_codes, w_sc, w_bf, slice(turn * N // 2, (turn + 1) * N // 2))
            put_lo(t1)
            if t1 != LAST_TILE:
                weigh_on_scalar(t1, ALL_QUERIES)

        gn_last = gn_t[:, LAST_TILE : LAST_TILE + 1]
        nc.vector.tensor_scalar(z_bf[:, HALVES[0], LAST_TILE], sd[LAST_TILE][:, HALVES[0]], gn_last, None, ALU.mult)
        weigh_on_scalar(LAST_TILE, HALVES[1])

        for cols in HALVES:
            quantise(z_codes, z_sc, z_bf, cols)
        for cols in HALVES:
            for m in range(N // P):
                rows = slice(m * P, (m + 1) * P)
                bank = psum.tile([P, S], F32, name="bank")
                nc.tensor.matmul_mx(
                    out=bank[:, 0:HALF],
                    lhsT=w_codes[:, rows].bitcast(FP8X4),
                    lhsT_scale=w_sc[:, rows],
                    rhs=z_codes[:, cols].bitcast(FP8X4),
                    rhs_scale=z_sc[:, cols],
                    start=True,
                    stop=True,
                )
                staged = stores.tile([P, HALF], F32, name="staged")
                if m % 2 == 0:
                    nc.scalar.copy(staged[:], bank[:, 0:HALF])
                else:
                    nc.vector.tensor_copy(staged[:], bank[:, 0:HALF])
                nc.sync.dma_start(out[rows, cols], staged[:])
